import numpy as np
import ml_dtypes

BF16 = ml_dtypes.bfloat16


def bf(x):
    return np.asarray(x, np.float32).astype(BF16)


def f32(x):
    return np.asarray(x, np.float32)


def f64(x):
    return np.asarray(x).astype(np.float64)


def striped(idx):
    return np.tile(idx.reshape(-1, 16).T, (8, 1))


S, K, M, N = 1024, 256, 128, 256


def setup_inputs():
    return {"table": bf(np.random.standard_normal((K, S))), "w": bf(np.random.standard_normal((K, M)) / np.sqrt(K)), "s": f32(0.5 + np.random.random_sample((M, 1))), "b": f32(0.5 * np.random.standard_normal((M, 1))), "offs": striped(np.random.permutation(np.tile(np.arange(S), 2))[:N])}


def reference(table, w, s, b, offs):
    idx = offs[:16].T.reshape(-1)
    x = f64(table)[:, idx]
    y = f64(w).T @ x
    return y * f64(s) + f64(b)

@@ -1,0 +1,46 @@
+import concourse.mybir as mybir
+
+BF16, F32, U16 = mybir.dt.bfloat16, mybir.dt.float32, mybir.dt.uint16
+MULT, ADD = mybir.AluOpType.mult, mybir.AluOpType.add
+
+P = 128
+K, S, M, N = 256, 1024, 128, 256
+K_BLOCKS = K // P
+
+FLOPS = 2 * K * M * N
+
+
+def tile_gather_matmul_kernel(tc, table, w, s, b, offs, out):
+    nc = tc.nc
+    with (
+        tc.tile_pool(name="held", bufs=1) as held,
+        tc.psum_pool(name="psum", bufs=1) as psum,
+    ):
+        offsets = held.tile([P, N // 16], U16, name="offsets")
+        nc.sync.dma_start(offsets[:], offs)
+        table_blocks = []
+        for kb in range(K_BLOCKS):
+            block = held.tile([P, S], BF16, name=f"table{kb}")
+            nc.sync.dma_start(block[:], table[kb * P : (kb + 1) * P, :])
+            table_blocks.append(block)
+
+        weights = held.tile([P, K_BLOCKS, M], BF16, name="weights")
+        nc.scalar.dma_start(weights[:], w.rearrange("(kb p) m -> p kb m", p=P))
+        gain = held.tile([M, 1], F32, name="gain")
+        nc.scalar.dma_start(gain[:], s)
+        shift = held.tile([M, 1], F32, name="shift")
+        nc.scalar.dma_start(shift[:], b)
+
+        y = psum.tile([M, N], F32, name="y")
+        for kb in range(K_BLOCKS):
+            nc.tensor.matmul(
+                y[:],
+                weights[:, kb, :],
+                table_blocks[kb][:].indirect(offsets[:]),
+                start=(kb == 0),
+                stop=(kb == K_BLOCKS - 1),
+            )
+
+        result = held.tile([M, N], F32, name="result")
+        nc.vector.tensor_scalar(result[:], y[:], gain[:, 0:1], shift[:, 0:1], MULT, ADD)
+        nc.sync.dma_start(out, result[:])

@@ -9,6 +9,9 @@ K_BLOCKS = K // P
 
 FLOPS = 2 * K * M * N
 
+WARM_COLUMNS = 512
+WARM_MATMULS = 4
+
 
 def tile_gather_matmul_kernel(tc, table, w, s, b, offs, out):
     nc = tc.nc
@@ -30,6 +33,12 @@ def tile_gather_matmul_kernel(tc, table, w, s, b, offs, out):
         nc.scalar.dma_start(gain[:], s)
         shift = held.tile([M, 1], F32, name="shift")
         nc.scalar.dma_start(shift[:], b)
+
+        zeros = held.tile([P, WARM_COLUMNS], BF16, name="zeros")
+        nc.vector.memset(zeros[:], 0.0)
+        unused = psum.tile([P, WARM_COLUMNS], F32, name="unused")
+        for _ in range(WARM_MATMULS):
+            nc.tensor.matmul(unused[:], zeros[:, 0:P], zeros[:], start=True, stop=True)
 
         y = psum.tile([M, N], F32, name="y")
         for kb in range(K_BLOCKS):

@@ -9,9 +9,6 @@ K_BLOCKS = K // P
 
 FLOPS = 2 * K * M * N
 
-WARM_COLUMNS = 512
-WARM_MATMULS = 4
-
 
 def tile_gather_matmul_kernel(tc, table, w, s, b, offs, out):
     nc = tc.nc
@@ -29,16 +26,11 @@ def tile_gather_matmul_kernel(tc, table, w, s, b, offs, out):
 
         weights = held.tile([P, K_BLOCKS, M], BF16, name="weights")
         nc.scalar.dma_start(weights[:], w.rearrange("(kb p) m -> p kb m", p=P))
-        gain = held.tile([M, 1], F32, name="gain")
-        nc.scalar.dma_start(gain[:], s)
-        shift = held.tile([M, 1], F32, name="shift")
-        nc.scalar.dma_start(shift[:], b)
 
-        zeros = held.tile([P, WARM_COLUMNS], BF16, name="zeros")
-        nc.vector.memset(zeros[:], 0.0)
-        unused = psum.tile([P, WARM_COLUMNS], F32, name="unused")
-        for _ in range(WARM_MATMULS):
-            nc.tensor.matmul(unused[:], zeros[:, 0:P], zeros[:], start=True, stop=True)
+        gain = held.tile([M, 1], F32, name="gain")
+        nc.gpsimd.dma_start(gain[:], s)
+        shift = held.tile([M, 1], F32, name="shift")
+        nc.gpsimd.dma_start(shift[:], b)
 
         y = psum.tile([M, N], F32, name="y")
         for kb in range(K_BLOCKS):

@@ -6,6 +6,7 @@ MULT, ADD = mybir.AluOpType.mult, mybir.AluOpType.add
 P = 128
 K, S, M, N = 256, 1024, 128, 256
 K_BLOCKS = K // P
+PIECES = 2
 
 FLOPS = 2 * K * M * N
 
@@ -26,22 +27,24 @@ def tile_gather_matmul_kernel(tc, table, w, s, b, offs, out):
 
         weights = held.tile([P, K_BLOCKS, M], BF16, name="weights")
         nc.scalar.dma_start(weights[:], w.rearrange("(kb p) m -> p kb m", p=P))
-
         gain = held.tile([M, 1], F32, name="gain")
-        nc.gpsimd.dma_start(gain[:], s)
+        nc.scalar.dma_start(gain[:], s)
         shift = held.tile([M, 1], F32, name="shift")
-        nc.gpsimd.dma_start(shift[:], b)
+        nc.scalar.dma_start(shift[:], b)
 
-        y = psum.tile([M, N], F32, name="y")
+        piece = N // PIECES
+        y = [psum.tile([M, piece], F32, name=f"y{p}") for p in range(PIECES)]
         for kb in range(K_BLOCKS):
-            nc.tensor.matmul(
-                y[:],
-                weights[:, kb, :],
-                table_blocks[kb][:].indirect(offsets[:]),
-                start=(kb == 0),
-                stop=(kb == K_BLOCKS - 1),
-            )
+            for p in range(PIECES):
+                nc.tensor.matmul(
+                    y[p][:],
+                    weights[:, kb, :],
+                    table_blocks[kb][:].indirect(offsets[:, p * (piece // 16) : (p + 1) * (piece // 16)]),
+                    start=(kb == 0),
+                    stop=(kb == K_BLOCKS - 1),
+                )
 
-        result = held.tile([M, N], F32, name="result")
-        nc.vector.tensor_scalar(result[:], y[:], gain[:, 0:1], shift[:, 0:1], MULT, ADD)
-        nc.sync.dma_start(out, result[:])
+        for p, queue in enumerate((nc.sync, nc.scalar)):
+            result = held.tile([M, piece], F32, name=f"result{p}")
+            nc.vector.tensor_scalar(result[:], y[p][:], gain[:, 0:1], shift[:, 0:1], MULT, ADD)
+            queue.dma_start(out[:, p * piece : (p + 1) * piece], result[:])

@@ -44,7 +44,7 @@ def tile_gather_matmul_kernel(tc, table, w, s, b, offs, out):
                     stop=(kb == K_BLOCKS - 1),
                 )
 
-        for p, queue in enumerate((nc.sync, nc.scalar)):
+        for p, queue in enumerate((nc.scalar, nc.sync)):
             result = held.tile([M, piece], F32, name=f"result{p}")
             nc.vector.tensor_scalar(result[:], y[p][:], gain[:, 0:1], shift[:, 0:1], MULT, ADD)
             queue.dma_start(out[:, p * piece : (p + 1) * piece], result[:])

@@ -7,6 +7,7 @@ P = 128
 K, S, M, N = 256, 1024, 128, 256
 K_BLOCKS = K // P
 PIECES = 2
+WARM_MATMULS, WARM_COLUMNS = 4, 512
 
 FLOPS = 2 * K * M * N
 
@@ -31,6 +32,12 @@ def tile_gather_matmul_kernel(tc, table, w, s, b, offs, out):
         nc.scalar.dma_start(gain[:], s)
         shift = held.tile([M, 1], F32, name="shift")
         nc.scalar.dma_start(shift[:], b)
+
+        zeros = held.tile([P, P], BF16, name="zeros")
+        nc.vector.memset(zeros[:], 0.0)
+        warm_out = psum.tile([P, WARM_COLUMNS], F32, name="warm_out")
+        for _ in range(WARM_MATMULS):
+            nc.tensor.matmul(warm_out[:], zeros[:], zeros[:, 0:1].to_broadcast([P, WARM_COLUMNS]), start=True, stop=True)
 
         piece = N // PIECES
         y = [psum.tile([M, piece], F32, name=f"y{p}") for p in range(PIECES)]

@@ -18,20 +18,20 @@ def tile_gather_matmul_kernel(tc, table, w, s, b, offs, out):
         tc.tile_pool(name="held", bufs=1) as held,
         tc.psum_pool(name="psum", bufs=1) as psum,
     ):
-        offsets = held.tile([P, N // 16], U16, name="offsets")
-        nc.sync.dma_start(offsets[:], offs)
         table_blocks = []
         for kb in range(K_BLOCKS):
             block = held.tile([P, S], BF16, name=f"table{kb}")
-            nc.sync.dma_start(block[:], table[kb * P : (kb + 1) * P, :])
+            nc.scalar.dma_start(block[:], table[kb * P : (kb + 1) * P, :])
             table_blocks.append(block)
-
-        weights = held.tile([P, K_BLOCKS, M], BF16, name="weights")
-        nc.scalar.dma_start(weights[:], w.rearrange("(kb p) m -> p kb m", p=P))
         gain = held.tile([M, 1], F32, name="gain")
         nc.scalar.dma_start(gain[:], s)
+
+        offsets = held.tile([P, N // 16], U16, name="offsets")
+        nc.sync.dma_start(offsets[:], offs)
+        weights = held.tile([P, K_BLOCKS, M], BF16, name="weights")
+        nc.sync.dma_start(weights[:], w.rearrange("(kb p) m -> p kb m", p=P))
         shift = held.tile([M, 1], F32, name="shift")
-        nc.scalar.dma_start(shift[:], b)
+        nc.sync.dma_start(shift[:], b)
 
         zeros = held.tile([P, P], BF16, name="zeros")
         nc.vector.memset(zeros[:], 0.0)

@@ -26,10 +26,10 @@ def tile_gather_matmul_kernel(tc, table, w, s, b, offs, out):
         gain = held.tile([M, 1], F32, name="gain")
         nc.scalar.dma_start(gain[:], s)
 
-        offsets = held.tile([P, N // 16], U16, name="offsets")
-        nc.sync.dma_start(offsets[:], offs)
         weights = held.tile([P, K_BLOCKS, M], BF16, name="weights")
         nc.sync.dma_start(weights[:], w.rearrange("(kb p) m -> p kb m", p=P))
+        offsets = held.tile([P, N // 16], U16, name="offsets")
+        nc.sync.dma_start(offsets[:], offs)
         shift = held.tile([M, 1], F32, name="shift")
         nc.sync.dma_start(shift[:], b)
 

import concourse.mybir as mybir

BF16, F32, U16 = mybir.dt.bfloat16, mybir.dt.float32, mybir.dt.uint16
MULT, ADD = mybir.AluOpType.mult, mybir.AluOpType.add

P = 128
K, S, M, N = 256, 1024, 128, 256
K_BLOCKS = K // P
PIECES = 2
WARM_MATMULS, WARM_COLUMNS = 4, 512

FLOPS = 2 * K * M * N


def tile_gather_matmul_kernel(tc, table, w, s, b, offs, out):
    nc = tc.nc
    with (
        tc.tile_pool(name="held", bufs=1) as held,
        tc.psum_pool(name="psum", bufs=1) as psum,
    ):
        table_blocks = []
        for kb in range(K_BLOCKS):
            block = held.tile([P, S], BF16, name=f"table{kb}")
            nc.scalar.dma_start(block[:], table[kb * P : (kb + 1) * P, :])
            table_blocks.append(block)
        gain = held.tile([M, 1], F32, name="gain")
        nc.scalar.dma_start(gain[:], s)

        weights = held.tile([P, K_BLOCKS, M], BF16, name="weights")
        nc.sync.dma_start(weights[:], w.rearrange("(kb p) m -> p kb m", p=P))
        offsets = held.tile([P, N // 16], U16, name="offsets")
        nc.sync.dma_start(offsets[:], offs)
        shift = held.tile([M, 1], F32, name="shift")
        nc.sync.dma_start(shift[:], b)

        zeros = held.tile([P, P], BF16, name="zeros")
        nc.vector.memset(zeros[:], 0.0)
        warm_out = psum.tile([P, WARM_COLUMNS], F32, name="warm_out")
        for _ in range(WARM_MATMULS):
            nc.tensor.matmul(warm_out[:], zeros[:], zeros[:, 0:1].to_broadcast([P, WARM_COLUMNS]), start=True, stop=True)

        piece = N // PIECES
        y = [psum.tile([M, piece], F32, name=f"y{p}") for p in range(PIECES)]
        for kb in range(K_BLOCKS):
            for p in range(PIECES):
                nc.tensor.matmul(
                    y[p][:],
                    weights[:, kb, :],
                    table_blocks[kb][:].indirect(offsets[:, p * (piece // 16) : (p + 1) * (piece // 16)]),
                    start=(kb == 0),
                    stop=(kb == K_BLOCKS - 1),
                )

        for p, queue in enumerate((nc.scalar, nc.sync)):
            result = held.tile([M, piece], F32, name=f"result{p}")
            nc.vector.tensor_scalar(result[:], y[p][:], gain[:, 0:1], shift[:, 0:1], MULT, ADD)
            queue.dma_start(out[:, p * piece : (p + 1) * piece], result[:])
